import numpy as np
import ml_dtypes


def mxq(x, axis, fmt="e4m3"):
    dtype, down = {"e4m3": (ml_dtypes.float8_e4m3fn, 7), "e5m2": (ml_dtypes.float8_e5m2, 14)}[fmt]
    v = np.moveaxis(np.asarray(x, np.float32).astype(ml_dtypes.bfloat16).astype(np.float64), axis, -1)
    blocks = v.reshape(v.shape[:-1] + (-1, 32))
    amax = np.abs(blocks).max(-1, keepdims=True)
    byte = np.maximum(np.where(amax > 0, np.frexp(amax)[1] - 1 + 127, 0) - down, 1)
    scale = np.exp2(byte - 127.0)
    codes = (blocks / scale).astype(np.float32).astype(dtype).astype(np.float64)
    return np.moveaxis((codes * scale).reshape(v.shape), -1, axis)


WIDE = False


def mx_kscale(k):
    if not WIDE:
        return np.ones(k)
    levels = np.array([30, -30])
    if k % 512:
        return np.exp2(np.random.permutation(np.resize(levels, k // 32))).repeat(32)
    a = np.empty((k // 512, 16))
    for p in range(k // 512):
        a[p, :8] = np.random.permutation(np.resize(levels, 8))
        for g in range(8):
            far = levels[np.abs(levels - a[p, g]) >= 10]
            a[p, g + 8] = far[np.random.randint(len(far))]
    return np.exp2(a.ravel()).repeat(32)


BF16 = ml_dtypes.bfloat16


def bf(x):
    return np.asarray(x, np.float32).astype(BF16)


def f64(x):
    return np.asarray(x).astype(np.float64)


E2M1 = np.array([0.0, 0.5, 1.0, 1.5, 2.0, 3.0, 4.0, 6.0, -0.0, -0.5, -1.0, -1.5, -2.0, -3.0, -4.0, -6.0])


def pack_weight(w, fmt):
    k, n = w.shape
    w = f64(bf(w)).reshape(k // 32, 32, n)
    amax = np.abs(w).max(1)
    if fmt == "e4m3":
        byte = np.frexp(amax)[1] - 1 + 127 - 7
    else:
        mant, ex = np.frexp(amax / 6.0)
        byte = np.where(mant > 0.5, ex, ex - 1) + 127
    byte = np.clip(np.where(amax > 0, byte, 1), 1, 254)
    scaled = (w * np.exp2(127.0 - byte)[:, None, :]).reshape(k, n).astype(np.float32)
    by_word = np.ascontiguousarray(scaled.reshape(k // 512, 128, 4, n).transpose(0, 1, 3, 2))
    if fmt == "e4m3":
        words = by_word.astype(ml_dtypes.float8_e4m3fn).view(np.uint8)
    else:
        c = by_word.astype(ml_dtypes.float4_e2m1fn).view(np.uint8) & 0xF
        words = c[..., 0::2] | (c[..., 1::2] << 4)
    return np.ascontiguousarray(words), np.ascontiguousarray(byte.astype(np.uint8).reshape(k // 512, 16, n))


def unpack_weight(words, scales, fmt):
    g, p, n, _ = words.shape
    if fmt == "e4m3":
        vals = np.ascontiguousarray(words).view(ml_dtypes.float8_e4m3fn).astype(np.float64)
    else:
        nib = np.empty((g, p, n, 4), np.uint8)
        nib[..., 0::2] = words & 0xF
        nib[..., 1::2] = words >> 4
        vals = E2M1[nib]
    vals = vals * np.repeat(np.exp2(scales.astype(np.float64) - 127.0), 8, axis=1)[..., None]
    return vals.transpose(0, 1, 3, 2).reshape(g * 512, n)
def pack4(w):
    words, scales = pack_weight(w, "e2m1")
    return words.reshape(words.shape[0], 128, -1), scales


def unpack4(words, scales):
    return unpack_weight(words.reshape(words.shape[0], 128, -1, 2), scales, "e2m1")


M, K, F, N = 1024, 1024, 2048, 1024

FLOOR = 0.1


def setup_inputs():
    s, t = mx_kscale(K), mx_kscale(F)
    up_words, up_scales = pack4(np.random.standard_normal((K, F)) / np.sqrt(K) / s[:, None] * t)
    pre = np.random.standard_normal((F, N))
    tune_a = np.random.standard_normal((F, N))
    tune_b = np.random.standard_normal((F, N))
    size = np.sqrt(1.0 / F) / t[:, None]
    return {"x": bf(np.random.standard_normal((M, K)) * s),
            "up_words": up_words,
            "up_scales": up_scales,
            "w_a": bf((pre + tune_a) * size),
            "w_b": bf((pre + tune_b) * size),
            "f_a": bf(FLOOR + np.random.standard_normal((F, N)) ** 2),
            "f_b": bf(FLOOR + np.random.standard_normal((F, N)) ** 2)}


def reference(x, up_words, up_scales, w_a, w_b, f_a, f_b):
    fa, fb = f64(f_a), f64(f_b)
    merged = (fa * f64(w_a) + fb * f64(w_b)) / (fa + fb)
    up = unpack4(up_words, up_scales)
    h = np.maximum(mxq(f64(x), 1, "e4m3") @ up, 0.0)
    return mxq(h, 1, "e5m2") @ mxq(merged, 0, "e4m3")

@@ -1,0 +1,248 @@
+from contextlib import ExitStack
+
+import concourse.mybir as mybir
+from concourse.masks import make_identity
+
+F32 = mybir.dt.float32
+BF16 = mybir.dt.bfloat16
+I32 = mybir.dt.int32
+U32 = mybir.dt.uint32
+U8 = mybir.dt.uint8
+E4M3 = mybir.dt.float8_e4m3fn_x4
+E5M2 = mybir.dt.float8_e5m2_x4
+E2M1 = mybir.dt.float4_e2m1fn_x4
+ACT = mybir.ActivationFunctionType
+
+M, K, F, N = 1024, 1024, 2048, 1024
+FLOPS = 2 * M * K * F + 2 * M * F * N
+
+P = 128
+KG = K // 512
+FG = F // 512
+MT = M // 128
+NH = N // 512
+
+
+STEPS = """
+    fa:1 fb:0 fb:1 x:1 La:1 fa:0 x:3 Lb:0 x:2 x:0 xT:1 upl La:0 xT:3 xT:2 xc:3:V xT:0 xc:2:V fb:2 Lb:1 S:0 
+    fa:2 fa:3 xc:1:A up xc:0:A x:6 Lb:2 fb:3 xq:0 wb:0 S:1 h:0:2 La:2 h:1:0 wa:0 h:0:3 wb:1 he:1:0:V h:1:2 
+    La:3 S:2 h:0:0 wa:1 wb:2 Lb:3 d:0 he:0:2:A d:1 wa:2 R:1 x:7 wb:3 S:3 fa:5 R:0 fb:4 xT:7 d:2 h:2:2 x:5 
+    h:1:1 x:4 he:0:0:A t:0 wb:4 he:1:1:A R:2 wa:4 xT:5 t:1 fa:4 h:1:3 he:0:3:A he:1:2:A wa:3 h:0:1 he:1:3:A 
+    h:3:1 D:0 he:0:1:A fb:5 xT:6 R:3 hq:1 d:3 xc:7:A La:4 xT:4 hq:0 D:1 Lb:4 Q:0 t:2 xc:5:A Lb:5 d:4 he:3:1:A 
+    fb:7 D:2 he:2:2:A xc:6:A h:2:3 wa:5 La:5 h:3:0 fa:6 t:3 h:2:0 h:3:3 wa:6 xc:4:A he:3:0:A Q:1 fa:7 he:2:0:A 
+    xq:1 he:2:3:A wb:6 La:6 S:4 h:5:1 wb:5 h:2:1 h:5:0 he:3:3:A fb:6 S:5 h:5:2 La:7 h:5:3 wb:7 h:3:2 h:4:2 D:3 
+    he:3:2:A h:4:0 Lb:6 hq:3 d:6 he:5:2:A he:5:0:A he:5:1:A he:5:3:A Q:3 h:7:2 he:2:1:A hq:5 Lb:7 h:4:3 hq:2 
+    d:5 h:7:0 h:6:0 he:4:0:A h:4:1 R:4 h:7:3 S:6 wa:7 S:7 he:4:2:A R:5 h:7:1 t:4 h:6:2 he:4:1:A Q:2 he:4:3:A 
+    t:5 he:7:2:A he:7:0:A h:6:3 he:7:1:A m:0:0:0 h:6:1 R:7 hq:4 m:0:0:1 D:4 m:0:0:2 he:6:0:A he:6:3:A m:5:0:0 
+    D:5 m:4:0:0 he:7:3:A he:6:2:A m:1:0:0 m:0:0:3 he:6:1:A R:6 hq:7 Q:5 m:7:0:0 m:1:0:1 hq:6 m:2:0:0 m:1:0:2 
+    Q:4 m:4:0:1 oe:0:0:A m:5:0:1 t:6 m:3:0:0 m:6:0:0 m:3:0:1 m:7:0:1 m:3:0:2 m:7:0:2 m:4:0:2 m:3:0:3 d:7 
+    m:2:0:1 m:5:0:2 m:7:0:3 m:4:0:3 oe:7:0:A m:1:0:3 m:5:0:3 m:6:0:1 oe:5:0:A m:6:0:2 D:6 m:6:1:0 oe:4:0:A 
+    m:2:0:2 m:6:1:1 oe:1:0:A m:7:1:0 m:0:1:0 oe:3:0:A m:6:0:3 m:2:1:0 oe:6:0:A t:7 m:2:0:3 m:3:1:0 oe:2:0:A 
+    m:2:1:1 m:7:1:1 m:1:1:0 m:4:1:0 m:0:1:1 m:5:1:0 Q:6 m:5:1:1 m:3:1:1 D:7 m:5:1:2 m:1:1:1 m:3:1:2 m:0:1:2 
+    m:6:1:2 m:7:1:2 m:4:1:1 m:1:1:2 Q:7 m:2:1:2 m:4:1:2 m:0:1:3 m:7:1:3 oe:0:1:A m:3:1:3 oe:7:1:V m:6:1:3 
+    oe:3:1:A m:2:1:3 oe:6:1:V m:5:1:3 oe:2:1:A m:1:1:3 oe:5:1:V m:4:1:3 oe:1:1:A oe:4:1:V 
+"""
+
+def tile_fisher_merged_ffn_s9_kernel(tc, x, up_words, up_scales, w_a, w_b, f_a, f_b, out):
+    nc = tc.nc
+    with ExitStack() as ctx:
+        keep = ctx.enter_context(tc.tile_pool(name="keep", bufs=1))
+        pool = ctx.enter_context(tc.tile_pool(name="pool", bufs=2))
+        psum = ctx.enter_context(tc.psum_pool(name="psum", bufs=8))
+
+        ident = keep.tile([P, P], F32, name="ident")
+        warm = keep.tile([P, 2], F32, name="warm")
+        xq = keep.tile([P, 2, KG, 512], U32, name="xq", align_bytes=256)
+        xs = keep.tile([P, 2, KG, 512], U8, name="xs", align_bytes=256)
+        up_q = keep.tile([P, KG * F // 2], I32, name="up_q", align_bytes=256)
+        up_s = keep.tile([P, KG * F // 4], I32, name="up_s", align_bytes=256)
+        s_raw = keep.tile([P, KG * F // 4], I32, name="s_raw", align_bytes=256)
+        hq = keep.tile([P, MT, FG, 128], U32, name="hq", align_bytes=256)
+        hs = keep.tile([P, MT, FG, 128], U8, name="hs", align_bytes=256)
+        dq = keep.tile([P, NH, FG, 512], U32, name="dq", align_bytes=256)
+        ds = keep.tile([P, NH, FG, 512], U8, name="ds", align_bytes=256)
+
+        nc.vector.memset(warm[:], 1.0)
+        nc.scalar.activation(out=warm[:, 0:1], in_=warm[:, 1:2], func=ACT.Ln)
+        nc.gpsimd.memset(s_raw[:], 0)
+        make_identity(nc, ident[:])
+
+        xr, xg, xbank = {}, {}, {}
+        upr = {}
+        ld = {}
+        la, lb, dd, db = {}, {}, {}, {}
+        hbank, hb, obank = {}, {}, {}
+
+        def load_x(mt):
+            xr[mt] = pool.tile([P, 512], F32, name="xr", tag="row", bufs=6, align_bytes=256)
+            nc.sync.dma_start(out=xr[mt][:].bitcast(BF16), in_=x[128 * mt : 128 * (mt + 1), :])
+
+        def load_up():
+            upr[0] = pool.tile([P, KG, F // 2], I32, name="upr", tag="pre", bufs=2, align_bytes=256)
+            for g in range(KG):
+                nc.sync.dma_start(out=upr[0][:, g, :], in_=up_words[g].bitcast(I32))
+            sv = s_raw[:].rearrange("p (g n) -> p g n", g=KG)
+            for q in range(4):
+                nc.sync.dma_start(
+                    out=sv[32 * q : 32 * q + 4, :, :],
+                    in_=up_scales[:, 4 * q : 4 * q + 4, :].rearrange("g r n -> r g n").bitcast(I32),
+                )
+
+        def permute_up():
+            src = upr[0][:].rearrange("p g n -> p (g n)")
+            for b in range(KG * FG):
+                cols = slice(256 * b, 256 * (b + 1))
+                nc.vector.tensor_copy(
+                    out=up_q[:, cols].rearrange("p (t q i) -> p t q i", t=4, i=2),
+                    in_=src[:, cols].rearrange("p (q t i) -> p t q i", t=4, i=2),
+                )
+            nc.vector.tensor_copy(
+                out=up_s[:].rearrange("p (b t q) -> p b t q", t=4, q=32),
+                in_=s_raw[:].rearrange("p (b q t) -> p b t q", t=4, q=32),
+            )
+
+        def load_d(src, key, bufs, c):
+            G, h = c % FG, c // FG
+            t = pool.tile([P, 4, 512], BF16, name=key, tag=key, bufs=bufs, align_bytes=256)
+            ld[key, c] = t
+            rows = src[512 * G : 512 * (G + 1), 512 * h : 512 * (h + 1)].rearrange("(q t i) n -> i q t n", t=4, i=4)
+            for i in range(4):
+                nc.sync.dma_start(out=t[i:P:4, :, :], in_=rows[i])
+
+        def flat(key, c):
+            return ld[key, c][:].rearrange("p t n -> p (t n)")
+
+        def ln_a(c):
+            la[c] = pool.tile([P, 2048], F32, name="la", tag="la", bufs=5, align_bytes=256)
+            nc.scalar.activation(out=la[c][:], in_=flat("fa", c), func=ACT.Ln)
+
+        def ln_b(c):
+            lb[c] = pool.tile([P, 2048], F32, name="lb", tag="lb", bufs=2, align_bytes=256)
+            nc.scalar.activation(out=lb[c][:], in_=flat("fb", c), func=ACT.Ln)
+
+        def ratio(c):
+            nc.vector.tensor_sub(out=la[c][:], in0=la[c][:], in1=lb[c][:])
+
+        def sig(c):
+            nc.scalar.activation(out=la[c][:], in_=la[c][:], func=ACT.Sigmoid)
+
+        def diff(c):
+            dd[c] = pool.tile([P, 2048], F32, name="dd", tag="dd", bufs=3, align_bytes=256)
+            nc.vector.tensor_sub(out=dd[c][:], in0=flat("wa", c), in1=flat("wb", c))
+
+        def mulr(c):
+            nc.vector.tensor_mul(out=la[c][:], in0=la[c][:], in1=dd[c][:])
+
+        def merge(c):
+            db[c] = pool.tile([P, 2048], BF16, name="db", tag="db", bufs=2, align_bytes=256)
+            nc.vector.tensor_add(
+                out=db[c][:].rearrange("p (c i t) -> p c t i", i=4, t=4),
+                in0=la[c][:].rearrange("p (t c i) -> p c t i", t=4, i=4),
+                in1=flat("wb", c).rearrange("p (t c i) -> p c t i", t=4, i=4),
+            )
+
+        def quant_d(c):
+            G, h = c % FG, c // FG
+            nc.vector.quantize_mx(out=dq[:, h, G, :].bitcast(E4M3), scales=ds[:, h, G, :], in_=db[c][:])
+
+        def turn_x(mt):
+            b = psum.tile([P, 512], F32, name="bank", tag="bank")
+            xbank[mt] = b
+            for g in range(KG):
+                for u in range(2):
+                    nc.tensor.transpose(
+                        b[:, 128 * (2 * g + u) : 128 * (2 * g + u + 1)],
+                        xr[mt][:, 256 * g + u : 256 * (g + 1) : 2],
+                        ident[:],
+                    )
+
+        def copy_x(mt, e):
+            if mt // 4 not in xg:
+                xg[mt // 4] = pool.tile([P, KG, 512, 2], F32, name="xg", tag="pre", bufs=2, align_bytes=256)
+            o = xg[mt // 4][:, :, 128 * (mt % 4) : 128 * (mt % 4 + 1), :]
+            i = xbank[mt][:].rearrange("p (g u r) -> p g r u", g=KG, u=2)
+            if e == "A":
+                nc.scalar.copy(out=o, in_=i)
+            else:
+                nc.vector.tensor_copy(out=o, in_=i)
+
+        def quant_x(mh):
+            nc.vector.quantize_mx(
+                out=xq[:, mh].rearrange("p g m -> p (g m)").bitcast(E4M3),
+                scales=xs[:, mh].rearrange("p g m -> p (g m)"),
+                in_=xg[mh][:].rearrange("p g m u -> p (g m u)").bitcast(BF16),
+            )
+
+        def up_mm(mt, G):
+            b = psum.tile([P, 512], F32, name="bank", tag="bank")
+            hbank[mt, G] = b
+            mcols = slice(128 * (mt % 4), 128 * (mt % 4 + 1))
+            for t in range(4):
+                for g in range(KG):
+                    blk = (g * FG + G) * 4 + t
+                    nc.tensor.matmul_mx(
+                        out=b[:, 128 * t : 128 * (t + 1)],
+                        lhsT=up_q[:, 64 * blk : 64 * (blk + 1)].bitcast(U8).bitcast(E2M1),
+                        lhsT_scale=up_s[:, 32 * blk : 32 * (blk + 1)].bitcast(U8),
+                        rhs=xq[:, mt // 4, g, mcols].bitcast(E4M3),
+                        rhs_scale=xs[:, mt // 4, g, mcols],
+                        start=(g == 0),
+                        stop=(g == KG - 1),
+                    )
+
+        def relu(mt, G, e):
+            if mt not in hb:
+                hb[mt] = pool.tile([P, FG, 512], BF16, name="hb", tag="hb", bufs=2, align_bytes=256)
+            o = hb[mt][:, G, :].rearrange("p (m t) -> p m t", t=4)
+            i = hbank[mt, G][:].rearrange("p (t m) -> p m t", t=4)
+            if e == "A":
+                nc.scalar.activation(out=o, in_=i, func=ACT.Relu)
+            else:
+                nc.vector.tensor_scalar_max(o, i, 0.0)
+
+        def quant_h(mt):
+            nc.vector.quantize_mx(
+                out=hq[:, mt].rearrange("p g m -> p (g m)").bitcast(E5M2),
+                scales=hs[:, mt].rearrange("p g m -> p (g m)"),
+                in_=hb[mt][:].rearrange("p g m -> p (g m)"),
+            )
+
+        def down_mm(mt, h, G):
+            if G == 0:
+                obank[mt, h] = psum.tile([P, 512], F32, name="bank", tag="bank")
+            nc.tensor.matmul_mx(
+                out=obank[mt, h][:],
+                lhsT=hq[:, mt, G, :].bitcast(E5M2),
+                lhsT_scale=hs[:, mt, G, :],
+                rhs=dq[:, h, G, :].bitcast(E4M3),
+                rhs_scale=ds[:, h, G, :],
+                start=(G == 0),
+                stop=(G == FG - 1),
+            )
+
+        def store(mt, h, e):
+            o = pool.tile([P, 512], F32, name="ob", tag="row", bufs=6, align_bytes=256)
+            if e == "A":
+                nc.scalar.copy(out=o[:], in_=obank[mt, h][:])
+            else:
+                nc.vector.tensor_copy(out=o[:], in_=obank[mt, h][:])
+            nc.sync.dma_start(out=out[128 * mt : 128 * (mt + 1), 512 * h : 512 * (h + 1)], in_=o[:])
+
+        do = {
+            "La": ln_a, "Lb": ln_b, "S": ratio, "R": sig, "d": diff, "t": mulr, "D": merge, "Q": quant_d,
+            "x": load_x, "xT": turn_x, "xc": copy_x, "xq": quant_x, "h": up_mm, "he": relu, "hq": quant_h,
+            "m": down_mm, "oe": store,
+        }
+        with tc.manual_schedule():
+            for step in STEPS.split():
+                parts = step.split(":")
+                name, args = parts[0], parts[1:]
+                if name in ("fa", "fb", "wa", "wb"):
+                    src, bufs = {"fa": (f_a, 2), "fb": (f_b, 2), "wa": (w_a, 2), "wb": (w_b, 5)}[name]
+                    load_d(src, name, bufs, int(args[0]))
+                elif name == "upl":
+                    load_up()
+                elif name == "up":
+                    permute_up()
+                else:
+                    do[name](*[a if a in "AV" else int(a) for a in args])

@@ -21,27 +21,29 @@ KG = K // 512
 FG = F // 512
 MT = M // 128
 NH = N // 512
+CHUNKS = [(0, 0), (0, 1), (1, 0), (1, 1), (2, 0), (3, 0), (2, 1), (3, 1)]
 
 
 STEPS = """
-    fa:1 fb:0 fb:1 x:1 La:1 fa:0 x:3 Lb:0 x:2 x:0 xT:1 upl La:0 xT:3 xT:2 xc:3:V xT:0 xc:2:V fb:2 Lb:1 S:0 
-    fa:2 fa:3 xc:1:A up xc:0:A x:6 Lb:2 fb:3 xq:0 wb:0 S:1 h:0:2 La:2 h:1:0 wa:0 h:0:3 wb:1 he:1:0:V h:1:2 
-    La:3 S:2 h:0:0 wa:1 wb:2 Lb:3 d:0 he:0:2:A d:1 wa:2 R:1 x:7 wb:3 S:3 fa:5 R:0 fb:4 xT:7 d:2 h:2:2 x:5 
-    h:1:1 x:4 he:0:0:A t:0 wb:4 he:1:1:A R:2 wa:4 xT:5 t:1 fa:4 h:1:3 he:0:3:A he:1:2:A wa:3 h:0:1 he:1:3:A 
-    h:3:1 D:0 he:0:1:A fb:5 xT:6 R:3 hq:1 d:3 xc:7:A La:4 xT:4 hq:0 D:1 Lb:4 Q:0 t:2 xc:5:A Lb:5 d:4 he:3:1:A 
-    fb:7 D:2 he:2:2:A xc:6:A h:2:3 wa:5 La:5 h:3:0 fa:6 t:3 h:2:0 h:3:3 wa:6 xc:4:A he:3:0:A Q:1 fa:7 he:2:0:A 
-    xq:1 he:2:3:A wb:6 La:6 S:4 h:5:1 wb:5 h:2:1 h:5:0 he:3:3:A fb:6 S:5 h:5:2 La:7 h:5:3 wb:7 h:3:2 h:4:2 D:3 
-    he:3:2:A h:4:0 Lb:6 hq:3 d:6 he:5:2:A he:5:0:A he:5:1:A he:5:3:A Q:3 h:7:2 he:2:1:A hq:5 Lb:7 h:4:3 hq:2 
-    d:5 h:7:0 h:6:0 he:4:0:A h:4:1 R:4 h:7:3 S:6 wa:7 S:7 he:4:2:A R:5 h:7:1 t:4 h:6:2 he:4:1:A Q:2 he:4:3:A 
-    t:5 he:7:2:A he:7:0:A h:6:3 he:7:1:A m:0:0:0 h:6:1 R:7 hq:4 m:0:0:1 D:4 m:0:0:2 he:6:0:A he:6:3:A m:5:0:0 
-    D:5 m:4:0:0 he:7:3:A he:6:2:A m:1:0:0 m:0:0:3 he:6:1:A R:6 hq:7 Q:5 m:7:0:0 m:1:0:1 hq:6 m:2:0:0 m:1:0:2 
-    Q:4 m:4:0:1 oe:0:0:A m:5:0:1 t:6 m:3:0:0 m:6:0:0 m:3:0:1 m:7:0:1 m:3:0:2 m:7:0:2 m:4:0:2 m:3:0:3 d:7 
-    m:2:0:1 m:5:0:2 m:7:0:3 m:4:0:3 oe:7:0:A m:1:0:3 m:5:0:3 m:6:0:1 oe:5:0:A m:6:0:2 D:6 m:6:1:0 oe:4:0:A 
-    m:2:0:2 m:6:1:1 oe:1:0:A m:7:1:0 m:0:1:0 oe:3:0:A m:6:0:3 m:2:1:0 oe:6:0:A t:7 m:2:0:3 m:3:1:0 oe:2:0:A 
-    m:2:1:1 m:7:1:1 m:1:1:0 m:4:1:0 m:0:1:1 m:5:1:0 Q:6 m:5:1:1 m:3:1:1 D:7 m:5:1:2 m:1:1:1 m:3:1:2 m:0:1:2 
-    m:6:1:2 m:7:1:2 m:4:1:1 m:1:1:2 Q:7 m:2:1:2 m:4:1:2 m:0:1:3 m:7:1:3 oe:0:1:A m:3:1:3 oe:7:1:V m:6:1:3 
-    oe:3:1:A m:2:1:3 oe:6:1:V m:5:1:3 oe:2:1:A m:1:1:3 oe:5:1:V m:4:1:3 oe:1:1:A oe:4:1:V 
+    fa:0:1 x:0 fb:0:0 x:1 La:1 fa:0:0 xT:0 x:2 xc:0:V fb:0:1 xq:0 Lb:0 xT:1 upl xc:1:V xq:1 xT:2 La:0 xc:2:V
+    x:3 xq:2 wa:0:0 Lb:1 S:0 wb:0:0 xT:3 x:4 up R:0 wa:0:1 x:5 S:1 h:1:3 fb:1 h:0:0 h:0:3 d:0 he:0:0:A xT:4
+    he:1:3:A h:1:2 x:6 he:0:3:A wb:0:1 h:0:2 xc:3:A h:2:2 xc:4:A xq:3 fa:1 h:1:1 t:0 R:1 h:0:1 h:2:3 h:1:0
+    fa:2 xq:4 he:0:2:A D:0 xT:5 he:1:1:A he:0:1:A he:1:0:A wa:1 he:1:2:A hq:0 Lb:2 d:1 xT:6 h:2:1 wb:1 xc:5:V
+    Q:0 t:1 he:2:2:A La:2 h:2:0 h:4:1 xq:5 h:3:3 hq:1 he:2:0:A D:1 La:3 S:2 he:2:3:A fb:2 Lb:3 h:3:0 h:5:3 Q:1
+    h:3:2 d:2 wb:2 xc:6:A he:2:1:A h:4:0 La:4 xq:6 hq:2 wa:2 d:3 he:4:1:A Lb:4 x:7 S:3 wa:3 he:3:0:A R:2 S:4
+    xT:7 fa:3 h:5:0 h:3:1 d:4 wb:3 he:4:0:A he:3:2:A t:2 he:3:1:A he:3:3:A R:3 h:6:2 hq:3 h:4:3 D:2 he:4:3:A
+    R:4 t:3 he:5:3:A xc:7:A h:4:2 Q:2 he:5:0:A h:6:0 xq:7 La:6 D:3 h:5:1 h:5:2 h:6:1 t:4 h:7:1 he:4:2:A fb:3
+    La:5 Q:3 hq:4 D:4 he:6:1:A he:6:2:A La:7 d:5 h:7:2 h:7:0 h:7:3 Lb:5 d:6 Lb:6 Q:4 S:5 he:5:1:A he:6:0:A d:7
+    he:5:2:A m:2:0:0 m:4:0:0 Lb:7 m:4:0:1 m:4:0:2 h:6:3 S:6 m:1:0:0 he:6:3:A R:5 hq:5 hq:6 S:7 he:7:3:A t:5
+    he:7:1:A he:7:0:A m:0:0:0 he:7:2:A R:6 m:6:0:0 hq:7 m:0:0:1 m:5:0:0 D:5 m:2:0:1 m:7:0:0 m:0:0:2 m:7:0:1
+    m:6:0:1 R:7 m:1:0:1 m:2:0:2 m:6:0:2 Q:5 m:5:0:1 m:1:0:2 t:6 m:7:0:2 m:2:0:3 m:4:0:3 oe:2:0:A m:0:0:3
+    m:6:0:3 oe:4:0:A m:7:0:3 m:3:0:0 oe:6:0:A m:1:0:3 m:1:1:0 D:6 oe:1:0:A m:5:0:2 m:6:1:0 oe:0:0:A m:5:0:3
+    m:3:0:1 oe:5:0:A m:3:0:2 m:4:1:0 oe:7:0:A m:4:1:1 t:7 m:5:1:0 m:2:1:0 m:6:1:1 m:3:0:3 m:2:1:1 oe:3:0:A
+    m:0:1:0 m:5:1:1 m:0:1:1 Q:6 m:3:1:0 m:7:1:0 m:3:1:1 D:7 m:7:1:1 m:1:1:1 m:2:1:2 m:7:1:2 m:5:1:2 m:0:1:2
+    m:1:1:2 m:4:1:2 m:6:1:2 Q:7 m:3:1:2 m:5:1:3 m:1:1:3 oe:5:1:V m:0:1:3 oe:1:1:A m:2:1:3 m:4:1:3 oe:0:1:A
+    oe:2:1:V m:6:1:3 m:7:1:3 oe:4:1:V oe:6:1:A m:3:1:3 oe:7:1:A oe:3:1:V
 """
+
 
 def tile_fisher_merged_ffn_s9_kernel(tc, x, up_words, up_scales, w_a, w_b, f_a, f_b, out):
     nc = tc.nc
@@ -52,11 +54,10 @@ def tile_fisher_merged_ffn_s9_kernel(tc, x, up_words, up_scales, w_a, w_b, f_a, 
 
         ident = keep.tile([P, P], F32, name="ident")
         warm = keep.tile([P, 2], F32, name="warm")
-        xq = keep.tile([P, 2, KG, 512], U32, name="xq", align_bytes=256)
-        xs = keep.tile([P, 2, KG, 512], U8, name="xs", align_bytes=256)
+        xq = keep.tile([P, MT, KG, 128], U32, name="xq", align_bytes=256)
+        xs = keep.tile([P, MT, KG, 128], U8, name="xs", align_bytes=256)
         up_q = keep.tile([P, KG * F // 2], I32, name="up_q", align_bytes=256)
         up_s = keep.tile([P, KG * F // 4], I32, name="up_s", align_bytes=256)
-        s_raw = keep.tile([P, KG * F // 4], I32, name="s_raw", align_bytes=256)
         hq = keep.tile([P, MT, FG, 128], U32, name="hq", align_bytes=256)
         hs = keep.tile([P, MT, FG, 128], U8, name="hs", align_bytes=256)
         dq = keep.tile([P, NH, FG, 512], U32, name="dq", align_bytes=256)
@@ -64,6 +65,7 @@ def tile_fisher_merged_ffn_s9_kernel(tc, x, up_words, up_scales, w_a, w_b, f_a, 
 
         nc.vector.memset(warm[:], 1.0)
         nc.scalar.activation(out=warm[:, 0:1], in_=warm[:, 1:2], func=ACT.Ln)
+        s_raw = pool.tile([P, KG * F // 4], I32, name="s_raw", tag="hb", bufs=2, align_bytes=256)
         nc.gpsimd.memset(s_raw[:], 0)
         make_identity(nc, ident[:])
 
@@ -74,11 +76,11 @@ def tile_fisher_merged_ffn_s9_kernel(tc, x, up_words, up_scales, w_a, w_b, f_a, 
         hbank, hb, obank = {}, {}, {}
 
         def load_x(mt):
-            xr[mt] = pool.tile([P, 512], F32, name="xr", tag="row", bufs=6, align_bytes=256)
+            xr[mt] = pool.tile([P, 512], F32, name="xr", tag="row", bufs=8, align_bytes=256)
             nc.sync.dma_start(out=xr[mt][:].bitcast(BF16), in_=x[128 * mt : 128 * (mt + 1), :])
 
         def load_up():
-            upr[0] = pool.tile([P, KG, F // 2], I32, name="upr", tag="pre", bufs=2, align_bytes=256)
+            upr[0] = pool.tile([P, KG, F // 2], I32, name="upr", tag="wa", bufs=2, align_bytes=256)
             for g in range(KG):
                 nc.sync.dma_start(out=upr[0][:, g, :], in_=up_words[g].bitcast(I32))
             sv = s_raw[:].rearrange("p (g n) -> p g n", g=KG)
@@ -89,36 +91,39 @@ def tile_fisher_merged_ffn_s9_kernel(tc, x, up_words, up_scales, w_a, w_b, f_a, 
                 )
 
         def permute_up():
-            src = upr[0][:].rearrange("p g n -> p (g n)")
-            for b in range(KG * FG):
-                cols = slice(256 * b, 256 * (b + 1))
+            for t in range(4):
                 nc.vector.tensor_copy(
-                    out=up_q[:, cols].rearrange("p (t q i) -> p t q i", t=4, i=2),
-                    in_=src[:, cols].rearrange("p (q t i) -> p t q i", t=4, i=2),
+                    out=up_q[:].rearrange("p (b t m) -> p b t m", t=4, m=64)[:, :, t, :].rearrange("p b (q i) -> p b q i", i=2),
+                    in_=upr[0][:].rearrange("p g (b q t i) -> p (g b) q t i", t=4, q=32, i=2)[:, :, :, t, :],
                 )
             nc.vector.tensor_copy(
                 out=up_s[:].rearrange("p (b t q) -> p b t q", t=4, q=32),
                 in_=s_raw[:].rearrange("p (b q t) -> p b t q", t=4, q=32),
             )
 
-        def load_d(src, key, bufs, c):
-            G, h = c % FG, c // FG
-            t = pool.tile([P, 4, 512], BF16, name=key, tag=key, bufs=bufs, align_bytes=256)
-            ld[key, c] = t
-            rows = src[512 * G : 512 * (G + 1), 512 * h : 512 * (h + 1)].rearrange("(q t i) n -> i q t n", t=4, i=4)
+        def load_d(key, G, h):
+            src, tag, bufs = {"fa": (f_a, "f", 3), "fb": (f_b, "f", 3), "wa": (w_a, "wa", 2), "wb": (w_b, "wb", 3)}[key]
+            if (key, G) not in ld:
+                ld[key, G] = pool.tile([P, 4, N], BF16, name=key, tag=tag, bufs=bufs, align_bytes=256)
+            cols = slice(0, N) if h is None else slice(512 * h, 512 * (h + 1))
+            rows = src[512 * G : 512 * (G + 1), cols].rearrange("(q t i) n -> i q t n", t=4, i=4)
             for i in range(4):
-                nc.sync.dma_start(out=t[i:P:4, :, :], in_=rows[i])
+                nc.sync.dma_start(out=ld[key, G][i:P:4, :, cols], in_=rows[i])
 
-        def flat(key, c):
-            return ld[key, c][:].rearrange("p t n -> p (t n)")
+        def half(key, c):
+            G, h = CHUNKS[c]
+            return ld[key, G][:, :, 512 * h : 512 * (h + 1)]
+
+        def rows4(tile):
+            return tile[:].rearrange("p (t n) -> p t n", t=4)
 
         def ln_a(c):
             la[c] = pool.tile([P, 2048], F32, name="la", tag="la", bufs=5, align_bytes=256)
-            nc.scalar.activation(out=la[c][:], in_=flat("fa", c), func=ACT.Ln)
+            nc.scalar.activation(out=rows4(la[c]), in_=half("fa", c), func=ACT.Ln)
 
         def ln_b(c):
             lb[c] = pool.tile([P, 2048], F32, name="lb", tag="lb", bufs=2, align_bytes=256)
-            nc.scalar.activation(out=lb[c][:], in_=flat("fb", c), func=ACT.Ln)
+            nc.scalar.activation(out=rows4(lb[c]), in_=half("fb", c), func=ACT.Ln)
 
         def ratio(c):
             nc.vector.tensor_sub(out=la[c][:], in0=la[c][:], in1=lb[c][:])
@@ -128,21 +133,21 @@ def tile_fisher_merged_ffn_s9_kernel(tc, x, up_words, up_scales, w_a, w_b, f_a, 
 
         def diff(c):
             dd[c] = pool.tile([P, 2048], F32, name="dd", tag="dd", bufs=3, align_bytes=256)
-            nc.vector.tensor_sub(out=dd[c][:], in0=flat("wa", c), in1=flat("wb", c))
+            nc.vector.tensor_sub(out=rows4(dd[c]), in0=half("wa", c), in1=half("wb", c))
 
         def mulr(c):
             nc.vector.tensor_mul(out=la[c][:], in0=la[c][:], in1=dd[c][:])
 
         def merge(c):
-            db[c] = pool.tile([P, 2048], BF16, name="db", tag="db", bufs=2, align_bytes=256)
+            db[c] = pool.tile([P, 2048], BF16, name="db", tag="db", bufs=1, align_bytes=256)
             nc.vector.tensor_add(
                 out=db[c][:].rearrange("p (c i t) -> p c t i", i=4, t=4),
                 in0=la[c][:].rearrange("p (t c i) -> p c t i", t=4, i=4),
-                in1=flat("wb", c).rearrange("p (t c i) -> p c t i", t=4, i=4),
+                in1=half("wb", c).rearrange("p t (c i) -> p c t i", i=4),
             )
 
         def quant_d(c):
-            G, h = c % FG, c // FG
+            G, h = CHUNKS[c]
             nc.vector.quantize_mx(out=dq[:, h, G, :].bitcast(E4M3), scales=ds[:, h, G, :], in_=db[c][:])
 
         def turn_x(mt):
@@ -157,26 +162,23 @@ def tile_fisher_merged_ffn_s9_kernel(tc, x, up_words, up_scales, w_a, w_b, f_a, 
                     )
 
         def copy_x(mt, e):
-            if mt // 4 not in xg:
-                xg[mt // 4] = pool.tile([P, KG, 512, 2], F32, name="xg", tag="pre", bufs=2, align_bytes=256)
-            o = xg[mt // 4][:, :, 128 * (mt % 4) : 128 * (mt % 4 + 1), :]
+            xg[mt] = pool.tile([P, KG, 128, 2], F32, name="xg", tag="row", bufs=8, align_bytes=256)
             i = xbank[mt][:].rearrange("p (g u r) -> p g r u", g=KG, u=2)
             if e == "A":
-                nc.scalar.copy(out=o, in_=i)
+                nc.scalar.copy(out=xg[mt][:], in_=i)
             else:
-                nc.vector.tensor_copy(out=o, in_=i)
+                nc.vector.tensor_copy(out=xg[mt][:], in_=i)
 
-        def quant_x(mh):
+        def quant_x(mt):
             nc.vector.quantize_mx(
-                out=xq[:, mh].rearrange("p g m -> p (g m)").bitcast(E4M3),
-                scales=xs[:, mh].rearrange("p g m -> p (g m)"),
-                in_=xg[mh][:].rearrange("p g m u -> p (g m u)").bitcast(BF16),
+                out=xq[:, mt].rearrange("p g m -> p (g m)").bitcast(E4M3),
+                scales=xs[:, mt].rearrange("p g m -> p (g m)"),
+                in_=xg[mt][:].rearrange("p g m u -> p (g m u)").bitcast(BF16),
             )
 
         def up_mm(mt, G):
             b = psum.tile([P, 512], F32, name="bank", tag="bank")
             hbank[mt, G] = b
-            mcols = slice(128 * (mt % 4), 128 * (mt % 4 + 1))
             for t in range(4):
                 for g in range(KG):
                     blk = (g * FG + G) * 4 + t
@@ -184,8 +186,8 @@ def tile_fisher_merged_ffn_s9_kernel(tc, x, up_words, up_scales, w_a, w_b, f_a, 
                         out=b[:, 128 * t : 128 * (t + 1)],
                         lhsT=up_q[:, 64 * blk : 64 * (blk + 1)].bitcast(U8).bitcast(E2M1),
                         lhsT_scale=up_s[:, 32 * blk : 32 * (blk + 1)].bitcast(U8),
-                        rhs=xq[:, mt // 4, g, mcols].bitcast(E4M3),
-                        rhs_scale=xs[:, mt // 4, g, mcols],
+                        rhs=xq[:, mt, g, :].bitcast(E4M3),
+                        rhs_scale=xs[:, mt, g, :],
                         start=(g == 0),
                         stop=(g == KG - 1),
                     )
@@ -221,7 +223,7 @@ def tile_fisher_merged_ffn_s9_kernel(tc, x, up_words, up_scales, w_a, w_b, f_a, 
             )
 
         def store(mt, h, e):
-            o = pool.tile([P, 512], F32, name="ob", tag="row", bufs=6, align_bytes=256)
+            o = pool.tile([P, 512], F32, name="ob", tag="row", bufs=8, align_bytes=256)
             if e == "A":
                 nc.scalar.copy(out=o[:], in_=obank[mt, h][:])
             else:
@@ -238,8 +240,7 @@ def tile_fisher_merged_ffn_s9_kernel(tc, x, up_words, up_scales, w_a, w_b, f_a, 
                 parts = step.split(":")
                 name, args = parts[0], parts[1:]
                 if name in ("fa", "fb", "wa", "wb"):
-                    src, bufs = {"fa": (f_a, 2), "fb": (f_b, 2), "wa": (w_a, 2), "wb": (w_b, 5)}[name]
-                    load_d(src, name, bufs, int(args[0]))
+                    load_d(name, int(args[0]), int(args[1]) if len(args) > 1 else None)
                 elif name == "upl":
                     load_up()
                 elif name == "up":

@@ -141,9 +141,9 @@ def tile_fisher_merged_ffn_s9_kernel(tc, x, up_words, up_scales, w_a, w_b, f_a, 
         def merge(c):
             db[c] = pool.tile([P, 2048], BF16, name="db", tag="db", bufs=1, align_bytes=256)
             nc.vector.tensor_add(
-                out=db[c][:].rearrange("p (c i t) -> p c t i", i=4, t=4),
-                in0=la[c][:].rearrange("p (t c i) -> p c t i", t=4, i=4),
-                in1=half("wb", c).rearrange("p t (c i) -> p c t i", i=4),
+                out=db[c][:].rearrange("p (c i t) -> p c t i", i=8, t=4),
+                in0=la[c][:].rearrange("p (t c i) -> p c t i", t=4, i=8),
+                in1=half("wb", c).rearrange("p t (c i) -> p c t i", i=8),
             )
 
         def quant_d(c):

@@ -1,4 +1,5 @@
 from contextlib import ExitStack
+from functools import partial
 
 import concourse.mybir as mybir
 from concourse.masks import make_identity
@@ -13,35 +14,39 @@ E5M2 = mybir.dt.float8_e5m2_x4
 E2M1 = mybir.dt.float4_e2m1fn_x4
 ACT = mybir.ActivationFunctionType
 
-M, K, F, N = 1024, 1024, 2048, 1024
-FLOPS = 2 * M * K * F + 2 * M * F * N
+TOKENS, K, F, N = 1024, 1024, 2048, 1024
+FLOPS = 2 * TOKENS * K * F + 2 * TOKENS * F * N
 
 P = 128
 KG = K // 512
 FG = F // 512
-MT = M // 128
-NH = N // 512
-CHUNKS = [(0, 0), (0, 1), (1, 0), (1, 1), (2, 0), (3, 0), (2, 1), (3, 1)]
+MT = TOKENS // 128
+COLS = 512
+NH = N // COLS
+BANKS_IN_PSUM = 8
 
+CHUNKS = [(G, h) for h in range(NH) for G in range(FG)]
 
-STEPS = """
-    fa:0:1 x:0 fb:0:0 x:1 La:1 fa:0:0 xT:0 x:2 xc:0:V fb:0:1 xq:0 Lb:0 xT:1 upl xc:1:V xq:1 xT:2 La:0 xc:2:V
-    x:3 xq:2 wa:0:0 Lb:1 S:0 wb:0:0 xT:3 x:4 up R:0 wa:0:1 x:5 S:1 h:1:3 fb:1 h:0:0 h:0:3 d:0 he:0:0:A xT:4
-    he:1:3:A h:1:2 x:6 he:0:3:A wb:0:1 h:0:2 xc:3:A h:2:2 xc:4:A xq:3 fa:1 h:1:1 t:0 R:1 h:0:1 h:2:3 h:1:0
-    fa:2 xq:4 he:0:2:A D:0 xT:5 he:1:1:A he:0:1:A he:1:0:A wa:1 he:1:2:A hq:0 Lb:2 d:1 xT:6 h:2:1 wb:1 xc:5:V
-    Q:0 t:1 he:2:2:A La:2 h:2:0 h:4:1 xq:5 h:3:3 hq:1 he:2:0:A D:1 La:3 S:2 he:2:3:A fb:2 Lb:3 h:3:0 h:5:3 Q:1
-    h:3:2 d:2 wb:2 xc:6:A he:2:1:A h:4:0 La:4 xq:6 hq:2 wa:2 d:3 he:4:1:A Lb:4 x:7 S:3 wa:3 he:3:0:A R:2 S:4
-    xT:7 fa:3 h:5:0 h:3:1 d:4 wb:3 he:4:0:A he:3:2:A t:2 he:3:1:A he:3:3:A R:3 h:6:2 hq:3 h:4:3 D:2 he:4:3:A
-    R:4 t:3 he:5:3:A xc:7:A h:4:2 Q:2 he:5:0:A h:6:0 xq:7 La:6 D:3 h:5:1 h:5:2 h:6:1 t:4 h:7:1 he:4:2:A fb:3
-    La:5 Q:3 hq:4 D:4 he:6:1:A he:6:2:A La:7 d:5 h:7:2 h:7:0 h:7:3 Lb:5 d:6 Lb:6 Q:4 S:5 he:5:1:A he:6:0:A d:7
-    he:5:2:A m:2:0:0 m:4:0:0 Lb:7 m:4:0:1 m:4:0:2 h:6:3 S:6 m:1:0:0 he:6:3:A R:5 hq:5 hq:6 S:7 he:7:3:A t:5
-    he:7:1:A he:7:0:A m:0:0:0 he:7:2:A R:6 m:6:0:0 hq:7 m:0:0:1 m:5:0:0 D:5 m:2:0:1 m:7:0:0 m:0:0:2 m:7:0:1
-    m:6:0:1 R:7 m:1:0:1 m:2:0:2 m:6:0:2 Q:5 m:5:0:1 m:1:0:2 t:6 m:7:0:2 m:2:0:3 m:4:0:3 oe:2:0:A m:0:0:3
-    m:6:0:3 oe:4:0:A m:7:0:3 m:3:0:0 oe:6:0:A m:1:0:3 m:1:1:0 D:6 oe:1:0:A m:5:0:2 m:6:1:0 oe:0:0:A m:5:0:3
-    m:3:0:1 oe:5:0:A m:3:0:2 m:4:1:0 oe:7:0:A m:4:1:1 t:7 m:5:1:0 m:2:1:0 m:6:1:1 m:3:0:3 m:2:1:1 oe:3:0:A
-    m:0:1:0 m:5:1:1 m:0:1:1 Q:6 m:3:1:0 m:7:1:0 m:3:1:1 D:7 m:7:1:1 m:1:1:1 m:2:1:2 m:7:1:2 m:5:1:2 m:0:1:2
-    m:1:1:2 m:4:1:2 m:6:1:2 Q:7 m:3:1:2 m:5:1:3 m:1:1:3 oe:5:1:V m:0:1:3 oe:1:1:A m:2:1:3 m:4:1:3 oe:0:1:A
-    oe:2:1:V m:6:1:3 m:7:1:3 oe:4:1:V oe:6:1:A m:3:1:3 oe:7:1:A oe:3:1:V
+BUFS = {"f": 5, "wa": 3, "wb": 5, "ratio": 5, "logb": 2, "diff": 4, "dbf": 1, "row": 8, "xt": 2, "h": 2}
+
+LOADS = """
+    fb0 fa0 x0 fa1 wa0 fb1 wb0 fa2 wa1 fb2 wb1 fb3 wb2 wa2 x1 x2 x3 fa3 fa4 fa5 x4 x5 wa3 up wa4 fb4 x6 fb5 x7 fa6 wb3
+    fa7 fb6 wb4 fb7 wb5 wa5 wb6 wa6 wb7 wa7
+"""
+VECTOR = """
+    cpx0 qx0 sub0 dif0 sub1 dif1 sub2 dif2 mul0 qx1 add0 mul1 qx2 qd0 mul2 qx3 perm add1 qx4 qd1 qx5 sub3 qx6 add2
+    dif3 sub4 qd2 qx7 dif4 sub5 qh0 dif5 dif6 sub6 sub7 mul3 qh1 add3 qh2 qd3 mul4 qh3 add4 dif7 qd4 qh4 mul5 qh5 add5
+    qh6 qd5 mul6 qh7 add6 mul7 qd6 add7 qd7
+"""
+BANKS = """
+    cpx0 cpx1 cpx2 cpx3 cpx4 cpx5 cpx6 relu0:0 relu0:1 relu0:2 cpx7 relu0:3 relu1:0 relu1:1 relu1:2 relu1:3 relu2:0
+    relu2:1 relu2:2 relu2:3 relu3:0 relu3:1 relu3:2 relu3:3 relu4:0 relu4:1 out0:0 relu4:2 relu4:3 out1:0 relu5:0
+    relu5:1 relu5:2 relu5:3 relu6:0 relu6:1 relu6:2 relu6:3 relu7:0 relu7:1 relu7:2 relu7:3 out2:0 out3:0 out4:0
+    out5:0 out6:0 out7:0
+"""
+SCALAR = """
+    lnb0+0 lna0+0 lna1+0 lnb1+0 lna2+0 lnb2+0 gate0+2 gate1+0 gate2+1 lna3+0 lnb3+2 lnb4+1 lna4+0 lna5+4 lna6+0 lnb5+0
+    lna7+1 lnb6+0 lnb7+1 gate3+7 gate4+6 gate5+12 gate6+5 gate7+5
 """
 
 
@@ -49,171 +54,158 @@ def tile_fisher_merged_ffn_s9_kernel(tc, x, up_words, up_scales, w_a, w_b, f_a, 
     nc = tc.nc
     with ExitStack() as ctx:
         keep = ctx.enter_context(tc.tile_pool(name="keep", bufs=1))
-        pool = ctx.enter_context(tc.tile_pool(name="pool", bufs=2))
-        psum = ctx.enter_context(tc.psum_pool(name="psum", bufs=8))
+        pool = ctx.enter_context(tc.tile_pool(name="pool", bufs=1))
+        psum = ctx.enter_context(tc.psum_pool(name="psum", bufs=BANKS_IN_PSUM))
 
         ident = keep.tile([P, P], F32, name="ident")
-        warm = keep.tile([P, 2], F32, name="warm")
+        first = keep.tile([P, 2], F32, name="first")
         xq = keep.tile([P, MT, KG, 128], U32, name="xq", align_bytes=256)
         xs = keep.tile([P, MT, KG, 128], U8, name="xs", align_bytes=256)
-        up_q = keep.tile([P, KG * F // 2], I32, name="up_q", align_bytes=256)
-        up_s = keep.tile([P, KG * F // 4], I32, name="up_s", align_bytes=256)
+        uq = keep.tile([P, KG * F // 2], I32, name="uq", align_bytes=256)
+        us = keep.tile([P, KG * F // 4], I32, name="us", align_bytes=256)
         hq = keep.tile([P, MT, FG, 128], U32, name="hq", align_bytes=256)
         hs = keep.tile([P, MT, FG, 128], U8, name="hs", align_bytes=256)
-        dq = keep.tile([P, NH, FG, 512], U32, name="dq", align_bytes=256)
-        ds = keep.tile([P, NH, FG, 512], U8, name="ds", align_bytes=256)
+        dq = keep.tile([P, NH, FG, COLS], U32, name="dq", align_bytes=256)
+        ds = keep.tile([P, NH, FG, COLS], U8, name="ds", align_bytes=256)
 
-        nc.vector.memset(warm[:], 1.0)
-        nc.scalar.activation(out=warm[:, 0:1], in_=warm[:, 1:2], func=ACT.Ln)
-        s_raw = pool.tile([P, KG * F // 4], I32, name="s_raw", tag="hb", bufs=2, align_bytes=256)
-        nc.gpsimd.memset(s_raw[:], 0)
+        def tile(name, shape, dtype, tag):
+            return pool.tile(shape, dtype, name=name, tag=tag, bufs=BUFS[tag], align_bytes=256)
+
+        nc.vector.memset(first[:], 1.0)
+        nc.scalar.activation(out=first[:, 0:1], in_=first[:, 1:2], func=ACT.Ln)
+        us_raw = tile("us_raw", [P, KG, F // 4], I32, "h")
+        nc.gpsimd.memset(us_raw[:].rearrange("p g n -> p (g n)"), 0)
+        uq_raw = tile("uq_raw", [P, KG, F // 2], I32, "ratio")
         make_identity(nc, ident[:])
 
-        xr, xg, xbank = {}, {}, {}
-        upr = {}
-        ld = {}
-        la, lb, dd, db = {}, {}, {}, {}
-        hbank, hb, obank = {}, {}, {}
+        wide = {"fa": (f_a, "f"), "fb": (f_b, "f"), "wa": (w_a, "wa"), "wb": (w_b, "wb")}
+        raw = {}
+        ratio, logb, diff, dbf, xt, hbf, bank = {}, {}, {}, {}, {}, {}, {}
+
+        def load_wide(key, c):
+            G, h = CHUNKS[c]
+            src, tag = wide[key]
+            raw[key + str(c)] = tile(key, [P, 4, COLS], BF16, tag)
+            view = src[512 * G : 512 * (G + 1), COLS * h : COLS * (h + 1)].rearrange("(q t i) n -> i q t n", t=4, i=4)
+            for i in range(4):
+                nc.sync.dma_start(out=raw[key + str(c)][i:P:4, :, :], in_=view[i])
 
         def load_x(mt):
-            xr[mt] = pool.tile([P, 512], F32, name="xr", tag="row", bufs=8, align_bytes=256)
-            nc.sync.dma_start(out=xr[mt][:].bitcast(BF16), in_=x[128 * mt : 128 * (mt + 1), :])
+            raw["x%d" % mt] = tile("xr", [P, K // 2], F32, "row")
+            nc.sync.dma_start(out=raw["x%d" % mt][:].bitcast(BF16), in_=x[128 * mt : 128 * (mt + 1), :])
 
         def load_up():
-            upr[0] = pool.tile([P, KG, F // 2], I32, name="upr", tag="wa", bufs=2, align_bytes=256)
             for g in range(KG):
-                nc.sync.dma_start(out=upr[0][:, g, :], in_=up_words[g].bitcast(I32))
-            sv = s_raw[:].rearrange("p (g n) -> p g n", g=KG)
+                nc.sync.dma_start(out=uq_raw[:, g, :], in_=up_words[g].bitcast(I32))
             for q in range(4):
-                nc.sync.dma_start(
-                    out=sv[32 * q : 32 * q + 4, :, :],
-                    in_=up_scales[:, 4 * q : 4 * q + 4, :].rearrange("g r n -> r g n").bitcast(I32),
-                )
+                view = up_scales[:, 4 * q : 4 * q + 4, :].rearrange("g r n -> r g n").bitcast(I32)
+                nc.sync.dma_start(out=us_raw[32 * q : 32 * q + 4, :, :], in_=view)
 
-        def permute_up():
-            for t in range(4):
-                nc.vector.tensor_copy(
-                    out=up_q[:].rearrange("p (b t m) -> p b t m", t=4, m=64)[:, :, t, :].rearrange("p b (q i) -> p b q i", i=2),
-                    in_=upr[0][:].rearrange("p g (b q t i) -> p (g b) q t i", t=4, q=32, i=2)[:, :, :, t, :],
-                )
-            nc.vector.tensor_copy(
-                out=up_s[:].rearrange("p (b t q) -> p b t q", t=4, q=32),
-                in_=s_raw[:].rearrange("p (b q t) -> p b t q", t=4, q=32),
-            )
-
-        def load_d(key, G, h):
-            src, tag, bufs = {"fa": (f_a, "f", 3), "fb": (f_b, "f", 3), "wa": (w_a, "wa", 2), "wb": (w_b, "wb", 3)}[key]
-            if (key, G) not in ld:
-                ld[key, G] = pool.tile([P, 4, N], BF16, name=key, tag=tag, bufs=bufs, align_bytes=256)
-            cols = slice(0, N) if h is None else slice(512 * h, 512 * (h + 1))
-            rows = src[512 * G : 512 * (G + 1), cols].rearrange("(q t i) n -> i q t n", t=4, i=4)
-            for i in range(4):
-                nc.sync.dma_start(out=ld[key, G][i:P:4, :, cols], in_=rows[i])
-
-        def half(key, c):
-            G, h = CHUNKS[c]
-            return ld[key, G][:, :, 512 * h : 512 * (h + 1)]
-
-        def rows4(tile):
-            return tile[:].rearrange("p (t n) -> p t n", t=4)
+        def by_row(t):
+            return t[:].rearrange("p (t n) -> p t n", t=4)
 
         def ln_a(c):
-            la[c] = pool.tile([P, 2048], F32, name="la", tag="la", bufs=5, align_bytes=256)
-            nc.scalar.activation(out=rows4(la[c]), in_=half("fa", c), func=ACT.Ln)
+            ratio[c] = tile("ratio", [P, 4 * COLS], F32, "ratio")
+            nc.scalar.activation(out=by_row(ratio[c]), in_=raw["fa%d" % c][:], func=ACT.Ln)
 
         def ln_b(c):
-            lb[c] = pool.tile([P, 2048], F32, name="lb", tag="lb", bufs=2, align_bytes=256)
-            nc.scalar.activation(out=rows4(lb[c]), in_=half("fb", c), func=ACT.Ln)
+            logb[c] = tile("logb", [P, 4 * COLS], F32, "logb")
+            nc.scalar.activation(out=by_row(logb[c]), in_=raw["fb%d" % c][:], func=ACT.Ln)
 
-        def ratio(c):
-            nc.vector.tensor_sub(out=la[c][:], in0=la[c][:], in1=lb[c][:])
+        def sub(c):
+            nc.vector.tensor_sub(out=ratio[c][:], in0=ratio[c][:], in1=logb[c][:])
 
-        def sig(c):
-            nc.scalar.activation(out=la[c][:], in_=la[c][:], func=ACT.Sigmoid)
+        def gate(c):
+            nc.scalar.activation(out=ratio[c][:], in_=ratio[c][:], func=ACT.Sigmoid)
 
-        def diff(c):
-            dd[c] = pool.tile([P, 2048], F32, name="dd", tag="dd", bufs=3, align_bytes=256)
-            nc.vector.tensor_sub(out=rows4(dd[c]), in0=half("wa", c), in1=half("wb", c))
+        def dif(c):
+            diff[c] = tile("diff", [P, 4 * COLS], F32, "diff")
+            nc.vector.tensor_sub(out=by_row(diff[c]), in0=raw["wa%d" % c][:], in1=raw["wb%d" % c][:])
 
-        def mulr(c):
-            nc.vector.tensor_mul(out=la[c][:], in0=la[c][:], in1=dd[c][:])
+        def mul(c):
+            nc.vector.tensor_mul(out=ratio[c][:], in0=ratio[c][:], in1=diff[c][:])
 
-        def merge(c):
-            db[c] = pool.tile([P, 2048], BF16, name="db", tag="db", bufs=1, align_bytes=256)
+        def add(c):
+            dbf[c] = tile("dbf", [P, 4 * COLS], BF16, "dbf")
             nc.vector.tensor_add(
-                out=db[c][:].rearrange("p (c i t) -> p c t i", i=8, t=4),
-                in0=la[c][:].rearrange("p (t c i) -> p c t i", t=4, i=8),
-                in1=half("wb", c).rearrange("p t (c i) -> p c t i", i=8),
+                out=dbf[c][:].rearrange("p (c i t) -> p c t i", i=8, t=4),
+                in0=ratio[c][:].rearrange("p (t c i) -> p c t i", t=4, i=8),
+                in1=raw["wb%d" % c][:].rearrange("p t (c i) -> p c t i", i=8),
             )
 
         def quant_d(c):
             G, h = CHUNKS[c]
-            nc.vector.quantize_mx(out=dq[:, h, G, :].bitcast(E4M3), scales=ds[:, h, G, :], in_=db[c][:])
+            nc.vector.quantize_mx(out=dq[:, h, G, :].bitcast(E4M3), scales=ds[:, h, G, :], in_=dbf[c][:])
+
+        def new_bank(name):
+            bank[name] = psum.tile([P, 512], F32, name="bank", tag="bank")
+            return bank[name]
 
         def turn_x(mt):
-            b = psum.tile([P, 512], F32, name="bank", tag="bank")
-            xbank[mt] = b
+            b = new_bank("cpx%d" % mt)
             for g in range(KG):
                 for u in range(2):
-                    nc.tensor.transpose(
-                        b[:, 128 * (2 * g + u) : 128 * (2 * g + u + 1)],
-                        xr[mt][:, 256 * g + u : 256 * (g + 1) : 2],
-                        ident[:],
-                    )
+                    cols = slice(128 * (2 * g + u), 128 * (2 * g + u + 1))
+                    nc.tensor.transpose(b[:, cols], raw["x%d" % mt][:, 256 * g + u : 256 * (g + 1) : 2], ident[:])
 
-        def copy_x(mt, e):
-            xg[mt] = pool.tile([P, KG, 128, 2], F32, name="xg", tag="row", bufs=8, align_bytes=256)
-            i = xbank[mt][:].rearrange("p (g u r) -> p g r u", g=KG, u=2)
-            if e == "A":
-                nc.scalar.copy(out=xg[mt][:], in_=i)
-            else:
-                nc.vector.tensor_copy(out=xg[mt][:], in_=i)
+        def copy_x(engine_copy, mt):
+            xt[mt] = tile("xt", [P, KG, 128, 2], F32, "xt")
+            engine_copy(out=xt[mt][:], in_=bank["cpx%d" % mt][:].rearrange("p (g u r) -> p g r u", g=KG, u=2))
 
         def quant_x(mt):
             nc.vector.quantize_mx(
                 out=xq[:, mt].rearrange("p g m -> p (g m)").bitcast(E4M3),
                 scales=xs[:, mt].rearrange("p g m -> p (g m)"),
-                in_=xg[mt][:].rearrange("p g m u -> p (g m u)").bitcast(BF16),
+                in_=xt[mt][:].rearrange("p g m u -> p (g m u)").bitcast(BF16),
+            )
+
+        def permute_up():
+            for t in range(4):
+                nc.vector.tensor_copy(
+                    out=uq[:].rearrange("p (b t m) -> p b t m", t=4, m=64)[:, :, t, :].rearrange("p b (q i) -> p b q i", i=2),
+                    in_=uq_raw[:].rearrange("p g (b q t i) -> p (g b) q t i", t=4, q=32, i=2)[:, :, :, t, :],
+                )
+            nc.vector.tensor_copy(
+                out=us[:].rearrange("p (b t q) -> p b t q", t=4, q=32),
+                in_=us_raw[:].rearrange("p g (b q t) -> p (g b) t q", t=4, q=32),
             )
 
         def up_mm(mt, G):
-            b = psum.tile([P, 512], F32, name="bank", tag="bank")
-            hbank[mt, G] = b
+            b = new_bank("relu%d:%d" % (mt, G))
             for t in range(4):
                 for g in range(KG):
-                    blk = (g * FG + G) * 4 + t
+                    place = 4 * (FG * g + G) + t
                     nc.tensor.matmul_mx(
                         out=b[:, 128 * t : 128 * (t + 1)],
-                        lhsT=up_q[:, 64 * blk : 64 * (blk + 1)].bitcast(U8).bitcast(E2M1),
-                        lhsT_scale=up_s[:, 32 * blk : 32 * (blk + 1)].bitcast(U8),
+                        lhsT=uq[:, 64 * place : 64 * (place + 1)].bitcast(U8).bitcast(E2M1),
+                        lhsT_scale=us[:, 32 * place : 32 * (place + 1)].bitcast(U8),
                         rhs=xq[:, mt, g, :].bitcast(E4M3),
                         rhs_scale=xs[:, mt, g, :],
                         start=(g == 0),
                         stop=(g == KG - 1),
                     )
 
-        def relu(mt, G, e):
-            if mt not in hb:
-                hb[mt] = pool.tile([P, FG, 512], BF16, name="hb", tag="hb", bufs=2, align_bytes=256)
-            o = hb[mt][:, G, :].rearrange("p (m t) -> p m t", t=4)
-            i = hbank[mt, G][:].rearrange("p (t m) -> p m t", t=4)
-            if e == "A":
-                nc.scalar.activation(out=o, in_=i, func=ACT.Relu)
-            else:
-                nc.vector.tensor_scalar_max(o, i, 0.0)
+        def relu(mt, G):
+            if mt not in hbf:
+                hbf[mt] = tile("hbf", [P, FG, 512], BF16, "h")
+            nc.scalar.activation(
+                out=hbf[mt][:, G, :].rearrange("p (m t) -> p m t", t=4),
+                in_=bank["relu%d:%d" % (mt, G)][:].rearrange("p (t m) -> p m t", t=4),
+                func=ACT.Relu,
+            )
 
         def quant_h(mt):
             nc.vector.quantize_mx(
                 out=hq[:, mt].rearrange("p g m -> p (g m)").bitcast(E5M2),
                 scales=hs[:, mt].rearrange("p g m -> p (g m)"),
-                in_=hb[mt][:].rearrange("p g m -> p (g m)"),
+                in_=hbf[mt][:].rearrange("p g m -> p (g m)"),
             )
 
         def down_mm(mt, h, G):
-            if G == 0:
-                obank[mt, h] = psum.tile([P, 512], F32, name="bank", tag="bank")
+            name = "out%d:%d" % (mt, h)
+            b = new_bank(name) if G == 0 else bank[name]
             nc.tensor.matmul_mx(
-                out=obank[mt, h][:],
+                out=b[:],
                 lhsT=hq[:, mt, G, :].bitcast(E5M2),
                 lhsT_scale=hs[:, mt, G, :],
                 rhs=dq[:, h, G, :].bitcast(E4M3),
@@ -222,28 +214,91 @@ def tile_fisher_merged_ffn_s9_kernel(tc, x, up_words, up_scales, w_a, w_b, f_a, 
                 stop=(G == FG - 1),
             )
 
-        def store(mt, h, e):
-            o = pool.tile([P, 512], F32, name="ob", tag="row", bufs=8, align_bytes=256)
-            if e == "A":
-                nc.scalar.copy(out=o[:], in_=obank[mt, h][:])
-            else:
-                nc.vector.tensor_copy(out=o[:], in_=obank[mt, h][:])
-            nc.sync.dma_start(out=out[128 * mt : 128 * (mt + 1), 512 * h : 512 * (h + 1)], in_=o[:])
+        def store(engine_copy, mt, h, pieces=1):
+            o = tile("o", [P, COLS], F32, "row")
+            width = COLS // pieces
+            for n in range(0, COLS, width):
+                engine_copy(out=o[:, n : n + width], in_=bank["out%d:%d" % (mt, h)][:, n : n + width])
+                to = out[128 * mt : 128 * (mt + 1), COLS * h + n : COLS * h + n + width]
+                nc.sync.dma_start(out=to, in_=o[:, n : n + width])
 
-        do = {
-            "La": ln_a, "Lb": ln_b, "S": ratio, "R": sig, "d": diff, "t": mulr, "D": merge, "Q": quant_d,
-            "x": load_x, "xT": turn_x, "xc": copy_x, "xq": quant_x, "h": up_mm, "he": relu, "hq": quant_h,
-            "m": down_mm, "oe": store,
-        }
+        loads = LOADS.split()
+        banks = BANKS.split()
+        vector = VECTOR.split()
+        on_vector = set(vector)
+
+        tensor = []
+        for name in banks:
+            tensor += ["down%s:%d" % (name[3:], G) for G in range(FG)] if name.startswith("out") else ["fill " + name]
+        for groups in ((0, 1), (2,), (3,)):
+            tensor += ["down%d:1:%d" % (mt, G) for mt in range(MT) for G in groups]
+
+        scalar = []
+        emptied = [name for name in banks if name not in on_vector]
+        for entry in SCALAR.split():
+            name, count = entry.split("+")
+            scalar += [name] + emptied[: int(count)]
+            emptied = emptied[int(count) :]
+        scalar += emptied
+
+        def engine_copy(name):
+            return nc.vector.tensor_copy if name in on_vector else nc.scalar.copy
+
+        steps = {"up": (load_up, []), "perm": (permute_up, ["up"])}
+        for c in range(len(CHUNKS)):
+            for key in wide:
+                steps["%s%d" % (key, c)] = (partial(load_wide, key, c), [])
+            steps["lna%d" % c] = (partial(ln_a, c), ["fa%d" % c])
+            steps["lnb%d" % c] = (partial(ln_b, c), ["fb%d" % c])
+            steps["sub%d" % c] = (partial(sub, c), ["lna%d" % c, "lnb%d" % c])
+            steps["gate%d" % c] = (partial(gate, c), ["sub%d" % c])
+            steps["dif%d" % c] = (partial(dif, c), ["wa%d" % c, "wb%d" % c])
+            steps["mul%d" % c] = (partial(mul, c), ["gate%d" % c, "dif%d" % c])
+            steps["add%d" % c] = (partial(add, c), ["mul%d" % c])
+            steps["qd%d" % c] = (partial(quant_d, c), ["add%d" % c])
+        for mt in range(MT):
+            name = "cpx%d" % mt
+            steps["x%d" % mt] = (partial(load_x, mt), [])
+            steps["fill " + name] = (partial(turn_x, mt), ["x%d" % mt])
+            steps[name] = (partial(copy_x, engine_copy(name), mt), ["fill " + name])
+            steps["qx%d" % mt] = (partial(quant_x, mt), [name])
+            for G in range(FG):
+                name = "relu%d:%d" % (mt, G)
+                steps["fill " + name] = (partial(up_mm, mt, G), ["qx%d" % mt, "perm"])
+                steps[name] = (partial(relu, mt, G), ["fill " + name])
+            steps["qh%d" % mt] = (partial(quant_h, mt), ["relu%d:%d" % (mt, G) for G in range(FG)])
+            for h in range(NH):
+                for G in range(FG):
+                    needs = ["qh%d" % mt, "qd%d" % CHUNKS.index((G, h))]
+                    steps["down%d:%d:%d" % (mt, h, G)] = (partial(down_mm, mt, h, G), needs)
+            name = "out%d:0" % mt
+            steps[name] = (partial(store, engine_copy(name), mt, 0), ["down%d:0:%d" % (mt, FG - 1)])
+
+        def takes(pairs, count):
+            for n in range(count, len(pairs)):
+                steps[pairs[n][0]][1].append(pairs[n - count][1])
+
+        reader = {"fa": "lna", "fb": "lnb", "wa": "dif", "wb": "add"}
+        for tag in ("f", "wa", "wb"):
+            takes([(n, reader[n[:2]] + n[2:]) for n in loads if wide.get(n[:2], ("", ""))[1] == tag], BUFS[tag])
+        takes([("cpx%d" % mt, "qx%d" % mt) for mt in range(MT)], BUFS["xt"])
+        takes([("up", "perm")] + [(n, "add" + n[3:]) for n in scalar if n.startswith("lna")], BUFS["ratio"])
+        takes([(n, "sub" + n[3:]) for n in scalar if n.startswith("lnb")], BUFS["logb"])
+        takes([(n, "mul" + n[3:]) for n in vector if n.startswith("dif")], BUFS["diff"])
+        takes([(n, "qd" + n[3:]) for n in vector if n.startswith("add")], BUFS["dbf"])
+        takes([("up", "perm")] + [("relu%d:0" % mt, "qh%d" % mt) for mt in range(MT)], BUFS["h"])
+        opens = [(n, n[5:] if n.startswith("fill") else "out" + n[4:-2]) for n in tensor if n.startswith("fill") or n[-2:] == ":0"]
+        takes(opens, BANKS_IN_PSUM)
+
+        queues = [loads, tensor, scalar, vector]
+        at = [0, 0, 0, 0]
+        issued = set()
         with tc.manual_schedule():
-            for step in STEPS.split():
-                parts = step.split(":")
-                name, args = parts[0], parts[1:]
-                if name in ("fa", "fb", "wa", "wb"):
-                    load_d(name, int(args[0]), int(args[1]) if len(args) > 1 else None)
-                elif name == "upl":
-                    load_up()
-                elif name == "up":
-                    permute_up()
-                else:
-                    do[name](*[a if a in "AV" else int(a) for a in args])
+            while len(issued) < len(steps):
+                ready = [e for e in range(4) if at[e] < len(queues[e]) and all(n in issued for n in steps[queues[e][at[e]]][1])]
+                name = queues[ready[0]][at[ready[0]]]
+                steps[name][0]()
+                issued.add(name)
+                at[ready[0]] += 1
+            for mt in range(MT):
+                store(nc.scalar.copy if mt % 2 == 0 else nc.vector.tensor_copy, mt, 1, pieces=2 if mt == 0 else 1)

from contextlib import ExitStack
from functools import partial

import concourse.mybir as mybir
from concourse.masks import make_identity

F32 = mybir.dt.float32
BF16 = mybir.dt.bfloat16
I32 = mybir.dt.int32
U32 = mybir.dt.uint32
U8 = mybir.dt.uint8
E4M3 = mybir.dt.float8_e4m3fn_x4
E5M2 = mybir.dt.float8_e5m2_x4
E2M1 = mybir.dt.float4_e2m1fn_x4
ACT = mybir.ActivationFunctionType

TOKENS, K, F, N = 1024, 1024, 2048, 1024
FLOPS = 2 * TOKENS * K * F + 2 * TOKENS * F * N

P = 128
KG = K // 512
FG = F // 512
MT = TOKENS // 128
COLS = 512
NH = N // COLS
BANKS_IN_PSUM = 8

CHUNKS = [(G, h) for h in range(NH) for G in range(FG)]

BUFS = {"f": 5, "wa": 3, "wb": 5, "ratio": 5, "logb": 2, "diff": 4, "dbf": 1, "row": 8, "xt": 2, "h": 2}

LOADS = """
    fb0 fa0 x0 fa1 wa0 fb1 wb0 fa2 wa1 fb2 wb1 fb3 wb2 wa2 x1 x2 x3 fa3 fa4 fa5 x4 x5 wa3 up wa4 fb4 x6 fb5 x7 fa6 wb3
    fa7 fb6 wb4 fb7 wb5 wa5 wb6 wa6 wb7 wa7
"""
VECTOR = """
    cpx0 qx0 sub0 dif0 sub1 dif1 sub2 dif2 mul0 qx1 add0 mul1 qx2 qd0 mul2 qx3 perm add1 qx4 qd1 qx5 sub3 qx6 add2
    dif3 sub4 qd2 qx7 dif4 sub5 qh0 dif5 dif6 sub6 sub7 mul3 qh1 add3 qh2 qd3 mul4 qh3 add4 dif7 qd4 qh4 mul5 qh5 add5
    qh6 qd5 mul6 qh7 add6 mul7 qd6 add7 qd7
"""
BANKS = """
    cpx0 cpx1 cpx2 cpx3 cpx4 cpx5 cpx6 relu0:0 relu0:1 relu0:2 cpx7 relu0:3 relu1:0 relu1:1 relu1:2 relu1:3 relu2:0
    relu2:1 relu2:2 relu2:3 relu3:0 relu3:1 relu3:2 relu3:3 relu4:0 relu4:1 out0:0 relu4:2 relu4:3 out1:0 relu5:0
    relu5:1 relu5:2 relu5:3 relu6:0 relu6:1 relu6:2 relu6:3 relu7:0 relu7:1 relu7:2 relu7:3 out2:0 out3:0 out4:0
    out5:0 out6:0 out7:0
"""
SCALAR = """
    lnb0+0 lna0+0 lna1+0 lnb1+0 lna2+0 lnb2+0 gate0+2 gate1+0 gate2+1 lna3+0 lnb3+2 lnb4+1 lna4+0 lna5+4 lna6+0 lnb5+0
    lna7+1 lnb6+0 lnb7+1 gate3+7 gate4+6 gate5+12 gate6+5 gate7+5
"""


def tile_fisher_merged_ffn_s9_kernel(tc, x, up_words, up_scales, w_a, w_b, f_a, f_b, out):
    nc = tc.nc
    with ExitStack() as ctx:
        keep = ctx.enter_context(tc.tile_pool(name="keep", bufs=1))
        pool = ctx.enter_context(tc.tile_pool(name="pool", bufs=1))
        psum = ctx.enter_context(tc.psum_pool(name="psum", bufs=BANKS_IN_PSUM))

        ident = keep.tile([P, P], F32, name="ident")
        first = keep.tile([P, 2], F32, name="first")
        xq = keep.tile([P, MT, KG, 128], U32, name="xq", align_bytes=256)
        xs = keep.tile([P, MT, KG, 128], U8, name="xs", align_bytes=256)
        uq = keep.tile([P, KG * F // 2], I32, name="uq", align_bytes=256)
        us = keep.tile([P, KG * F // 4], I32, name="us", align_bytes=256)
        hq = keep.tile([P, MT, FG, 128], U32, name="hq", align_bytes=256)
        hs = keep.tile([P, MT, FG, 128], U8, name="hs", align_bytes=256)
        dq = keep.tile([P, NH, FG, COLS], U32, name="dq", align_bytes=256)
        ds = keep.tile([P, NH, FG, COLS], U8, name="ds", align_bytes=256)

        def tile(name, shape, dtype, tag):
            return pool.tile(shape, dtype, name=name, tag=tag, bufs=BUFS[tag], align_bytes=256)

        nc.vector.memset(first[:], 1.0)
        nc.scalar.activation(out=first[:, 0:1], in_=first[:, 1:2], func=ACT.Ln)
        us_raw = tile("us_raw", [P, KG, F // 4], I32, "h")
        nc.gpsimd.memset(us_raw[:].rearrange("p g n -> p (g n)"), 0)
        uq_raw = tile("uq_raw", [P, KG, F // 2], I32, "ratio")
        make_identity(nc, ident[:])

        wide = {"fa": (f_a, "f"), "fb": (f_b, "f"), "wa": (w_a, "wa"), "wb": (w_b, "wb")}
        raw = {}
        ratio, logb, diff, dbf, xt, hbf, bank = {}, {}, {}, {}, {}, {}, {}

        def load_wide(key, c):
            G, h = CHUNKS[c]
            src, tag = wide[key]
            raw[key + str(c)] = tile(key, [P, 4, COLS], BF16, tag)
            view = src[512 * G : 512 * (G + 1), COLS * h : COLS * (h + 1)].rearrange("(q t i) n -> i q t n", t=4, i=4)
            for i in range(4):
                nc.sync.dma_start(out=raw[key + str(c)][i:P:4, :, :], in_=view[i])

        def load_x(mt):
            raw["x%d" % mt] = tile("xr", [P, K // 2], F32, "row")
            nc.sync.dma_start(out=raw["x%d" % mt][:].bitcast(BF16), in_=x[128 * mt : 128 * (mt + 1), :])

        def load_up():
            for g in range(KG):
                nc.sync.dma_start(out=uq_raw[:, g, :], in_=up_words[g].bitcast(I32))
            for q in range(4):
                view = up_scales[:, 4 * q : 4 * q + 4, :].rearrange("g r n -> r g n").bitcast(I32)
                nc.sync.dma_start(out=us_raw[32 * q : 32 * q + 4, :, :], in_=view)

        def by_row(t):
            return t[:].rearrange("p (t n) -> p t n", t=4)

        def ln_a(c):
            ratio[c] = tile("ratio", [P, 4 * COLS], F32, "ratio")
            nc.scalar.activation(out=by_row(ratio[c]), in_=raw["fa%d" % c][:], func=ACT.Ln)

        def ln_b(c):
            logb[c] = tile("logb", [P, 4 * COLS], F32, "logb")
            nc.scalar.activation(out=by_row(logb[c]), in_=raw["fb%d" % c][:], func=ACT.Ln)

        def sub(c):
            nc.vector.tensor_sub(out=ratio[c][:], in0=ratio[c][:], in1=logb[c][:])

        def gate(c):
            nc.scalar.activation(out=ratio[c][:], in_=ratio[c][:], func=ACT.Sigmoid)

        def dif(c):
            diff[c] = tile("diff", [P, 4 * COLS], F32, "diff")
            nc.vector.tensor_sub(out=by_row(diff[c]), in0=raw["wa%d" % c][:], in1=raw["wb%d" % c][:])

        def mul(c):
            nc.vector.tensor_mul(out=ratio[c][:], in0=ratio[c][:], in1=diff[c][:])

        def add(c):
            dbf[c] = tile("dbf", [P, 4 * COLS], BF16, "dbf")
            nc.vector.tensor_add(
                out=dbf[c][:].rearrange("p (c i t) -> p c t i", i=8, t=4),
                in0=ratio[c][:].rearrange("p (t c i) -> p c t i", t=4, i=8),
                in1=raw["wb%d" % c][:].rearrange("p t (c i) -> p c t i", i=8),
            )

        def quant_d(c):
            G, h = CHUNKS[c]
            nc.vector.quantize_mx(out=dq[:, h, G, :].bitcast(E4M3), scales=ds[:, h, G, :], in_=dbf[c][:])

        def new_bank(name):
            bank[name] = psum.tile([P, 512], F32, name="bank", tag="bank")
            return bank[name]

        def turn_x(mt):
            b = new_bank("cpx%d" % mt)
            for g in range(KG):
                for u in range(2):
                    cols = slice(128 * (2 * g + u), 128 * (2 * g + u + 1))
                    nc.tensor.transpose(b[:, cols], raw["x%d" % mt][:, 256 * g + u : 256 * (g + 1) : 2], ident[:])

        def copy_x(engine_copy, mt):
            xt[mt] = tile("xt", [P, KG, 128, 2], F32, "xt")
            engine_copy(out=xt[mt][:], in_=bank["cpx%d" % mt][:].rearrange("p (g u r) -> p g r u", g=KG, u=2))

        def quant_x(mt):
            nc.vector.quantize_mx(
                out=xq[:, mt].rearrange("p g m -> p (g m)").bitcast(E4M3),
                scales=xs[:, mt].rearrange("p g m -> p (g m)"),
                in_=xt[mt][:].rearrange("p g m u -> p (g m u)").bitcast(BF16),
            )

        def permute_up():
            for t in range(4):
                nc.vector.tensor_copy(
                    out=uq[:].rearrange("p (b t m) -> p b t m", t=4, m=64)[:, :, t, :].rearrange("p b (q i) -> p b q i", i=2),
                    in_=uq_raw[:].rearrange("p g (b q t i) -> p (g b) q t i", t=4, q=32, i=2)[:, :, :, t, :],
                )
            nc.vector.tensor_copy(
                out=us[:].rearrange("p (b t q) -> p b t q", t=4, q=32),
                in_=us_raw[:].rearrange("p g (b q t) -> p (g b) t q", t=4, q=32),
            )

        def up_mm(mt, G):
            b = new_bank("relu%d:%d" % (mt, G))
            for t in range(4):
                for g in range(KG):
                    place = 4 * (FG * g + G) + t
                    nc.tensor.matmul_mx(
                        out=b[:, 128 * t : 128 * (t + 1)],
                        lhsT=uq[:, 64 * place : 64 * (place + 1)].bitcast(U8).bitcast(E2M1),
                        lhsT_scale=us[:, 32 * place : 32 * (place + 1)].bitcast(U8),
                        rhs=xq[:, mt, g, :].bitcast(E4M3),
                        rhs_scale=xs[:, mt, g, :],
                        start=(g == 0),
                        stop=(g == KG - 1),
                    )

        def relu(mt, G):
            if mt not in hbf:
                hbf[mt] = tile("hbf", [P, FG, 512], BF16, "h")
            nc.scalar.activation(
                out=hbf[mt][:, G, :].rearrange("p (m t) -> p m t", t=4),
                in_=bank["relu%d:%d" % (mt, G)][:].rearrange("p (t m) -> p m t", t=4),
                func=ACT.Relu,
            )

        def quant_h(mt):
            nc.vector.quantize_mx(
                out=hq[:, mt].rearrange("p g m -> p (g m)").bitcast(E5M2),
                scales=hs[:, mt].rearrange("p g m -> p (g m)"),
                in_=hbf[mt][:].rearrange("p g m -> p (g m)"),
            )

        def down_mm(mt, h, G):
            name = "out%d:%d" % (mt, h)
            b = new_bank(name) if G == 0 else bank[name]
            nc.tensor.matmul_mx(
                out=b[:],
                lhsT=hq[:, mt, G, :].bitcast(E5M2),
                lhsT_scale=hs[:, mt, G, :],
                rhs=dq[:, h, G, :].bitcast(E4M3),
                rhs_scale=ds[:, h, G, :],
                start=(G == 0),
                stop=(G == FG - 1),
            )

        def store(engine_copy, mt, h, pieces=1):
            o = tile("o", [P, COLS], F32, "row")
            width = COLS // pieces
            for n in range(0, COLS, width):
                engine_copy(out=o[:, n : n + width], in_=bank["out%d:%d" % (mt, h)][:, n : n + width])
                to = out[128 * mt : 128 * (mt + 1), COLS * h + n : COLS * h + n + width]
                nc.sync.dma_start(out=to, in_=o[:, n : n + width])

        loads = LOADS.split()
        banks = BANKS.split()
        vector = VECTOR.split()
        on_vector = set(vector)

        tensor = []
        for name in banks:
            tensor += ["down%s:%d" % (name[3:], G) for G in range(FG)] if name.startswith("out") else ["fill " + name]
        for groups in ((0, 1), (2,), (3,)):
            tensor += ["down%d:1:%d" % (mt, G) for mt in range(MT) for G in groups]

        scalar = []
        emptied = [name for name in banks if name not in on_vector]
        for entry in SCALAR.split():
            name, count = entry.split("+")
            scalar += [name] + emptied[: int(count)]
            emptied = emptied[int(count) :]
        scalar += emptied

        def engine_copy(name):
            return nc.vector.tensor_copy if name in on_vector else nc.scalar.copy

        steps = {"up": (load_up, []), "perm": (permute_up, ["up"])}
        for c in range(len(CHUNKS)):
            for key in wide:
                steps["%s%d" % (key, c)] = (partial(load_wide, key, c), [])
            steps["lna%d" % c] = (partial(ln_a, c), ["fa%d" % c])
            steps["lnb%d" % c] = (partial(ln_b, c), ["fb%d" % c])
            steps["sub%d" % c] = (partial(sub, c), ["lna%d" % c, "lnb%d" % c])
            steps["gate%d" % c] = (partial(gate, c), ["sub%d" % c])
            steps["dif%d" % c] = (partial(dif, c), ["wa%d" % c, "wb%d" % c])
            steps["mul%d" % c] = (partial(mul, c), ["gate%d" % c, "dif%d" % c])
            steps["add%d" % c] = (partial(add, c), ["mul%d" % c])
            steps["qd%d" % c] = (partial(quant_d, c), ["add%d" % c])
        for mt in range(MT):
            name = "cpx%d" % mt
            steps["x%d" % mt] = (partial(load_x, mt), [])
            steps["fill " + name] = (partial(turn_x, mt), ["x%d" % mt])
            steps[name] = (partial(copy_x, engine_copy(name), mt), ["fill " + name])
            steps["qx%d" % mt] = (partial(quant_x, mt), [name])
            for G in range(FG):
                name = "relu%d:%d" % (mt, G)
                steps["fill " + name] = (partial(up_mm, mt, G), ["qx%d" % mt, "perm"])
                steps[name] = (partial(relu, mt, G), ["fill " + name])
            steps["qh%d" % mt] = (partial(quant_h, mt), ["relu%d:%d" % (mt, G) for G in range(FG)])
            for h in range(NH):
                for G in range(FG):
                    needs = ["qh%d" % mt, "qd%d" % CHUNKS.index((G, h))]
                    steps["down%d:%d:%d" % (mt, h, G)] = (partial(down_mm, mt, h, G), needs)
            name = "out%d:0" % mt
            steps[name] = (partial(store, engine_copy(name), mt, 0), ["down%d:0:%d" % (mt, FG - 1)])

        def takes(pairs, count):
            for n in range(count, len(pairs)):
                steps[pairs[n][0]][1].append(pairs[n - count][1])

        reader = {"fa": "lna", "fb": "lnb", "wa": "dif", "wb": "add"}
        for tag in ("f", "wa", "wb"):
            takes([(n, reader[n[:2]] + n[2:]) for n in loads if wide.get(n[:2], ("", ""))[1] == tag], BUFS[tag])
        takes([("cpx%d" % mt, "qx%d" % mt) for mt in range(MT)], BUFS["xt"])
        takes([("up", "perm")] + [(n, "add" + n[3:]) for n in scalar if n.startswith("lna")], BUFS["ratio"])
        takes([(n, "sub" + n[3:]) for n in scalar if n.startswith("lnb")], BUFS["logb"])
        takes([(n, "mul" + n[3:]) for n in vector if n.startswith("dif")], BUFS["diff"])
        takes([(n, "qd" + n[3:]) for n in vector if n.startswith("add")], BUFS["dbf"])
        takes([("up", "perm")] + [("relu%d:0" % mt, "qh%d" % mt) for mt in range(MT)], BUFS["h"])
        opens = [(n, n[5:] if n.startswith("fill") else "out" + n[4:-2]) for n in tensor if n.startswith("fill") or n[-2:] == ":0"]
        takes(opens, BANKS_IN_PSUM)

        queues = [loads, tensor, scalar, vector]
        at = [0, 0, 0, 0]
        issued = set()
        with tc.manual_schedule():
            while len(issued) < len(steps):
                ready = [e for e in range(4) if at[e] < len(queues[e]) and all(n in issued for n in steps[queues[e][at[e]]][1])]
                name = queues[ready[0]][at[ready[0]]]
                steps[name][0]()
                issued.add(name)
                at[ready[0]] += 1
            for mt in range(MT):
                store(nc.scalar.copy if mt % 2 == 0 else nc.vector.tensor_copy, mt, 1, pieces=2 if mt == 0 else 1)
